import numpy as np
CORES = [0,1,2,3,4,5,6,7,8,9,10,11,12,13,14,15,16,17,18,19,20,21,22,23,24,25,26,27,28,29,30,31,32,33,34,35,36,37,38,39,40,41,42,43,44,45,46,47,48,49,50,51,52,53,54,55,56,57,58,59,60,61,62,63,64,65,66,67,68,69,70,71,72,73,74,75,76,77,78,79,80,81,82,83,84,85,86,87,88,89,90,91,92,93,94,95,96,97,98,99,100,101,102,103,104,105,106,107,108,109,110,111,112,113,114,115,116,117,118,119,120,121,122,123,124,125,126,127,128,129,130,131,132,133,134,135,136,137,138,139,140,141,142,143,144,145,146,147,148,149,150,151,152,153,154,155,156,157,158,159,160,161,162,163,164,165,166,167,168,169,170,171,172,173,174,175,176,177,178,179,180,181,182,183,184,185,186,187,188,189,190,191,192,193,194,195,196,197,198,199,200,201,202,203,204,205,206,207,208,209,210,211,212,213,214,215,216,217,218,219,220,221,222,223,224,225,226,227,228,229,230,231,232,233,234,235,236,237,238,239,240,241,242,243,244,245,246,247,248,249,250,251,252,253,254,255,256,257,258,259,260,261,262,263,264,265,266,267,268,269,270,271,272,273,274,275,276,277,278,279,280,281,282,283,284,285,286,287,288,289,290,291,292,293,294,295,296,297,298,299,300,301,302,303,304,305,306,307,308,309,310,311,312,313,314,315,316,317,318,319,320,321,322,323,324,325,326,327,328,329,330,331,332,333,334,335,336,337,338,339,340,341,342,343,344,345,346,347,348,349,350,351,352,353,354,355,356,357,358,359,360,361,362,363,364,365,366,367,368,369,370,371,372,373,374,375,376,377,378,379,380,381,382,383,384,385,386,387,388,389,390,391,392,393,394,395,396,397,398,399,400,401,402,403,404,405,406,407,408,409,410,411,412,413,414,415,416,417,418,419,420,421,422,423,424,425,426,427,428,429,430,431,432,433,434,435,436,437,438,439,440,441,442,443,444,445,446,447,448,449,450,451,452,453,454,455,456,457,458,459,460,461,462,463,464,465,466,467,468,469,470,471,472,473,474,475,476,477,478,479,480,481,482,483,484,485,486,487,488,489,490,491,492,493,494,495,496,497,498,499,500,501,502,503,504,505,506,507,508,509,510,511]
N = 512
def setup_inputs(rng):
    return {"x": rng.standard_normal((N, 128, 1024), dtype=np.float32)}
def reference(x):
    s = x.sum(axis=0, dtype=np.float64).astype(x.dtype)
    b = 1024 // N
    return {"y": np.stack([s[:, r * b:(r + 1) * b] for r in range(N)])}

@@ -1,0 +1,114 @@
+import concourse.bass as bass
+from concourse.mybir import AluOpType
+
+PORT = (2, 3, 6, 7)
+PLAIN = (0, 1, 4, 5)
+
+SCRATCH = {
+    "xs": ("sbuf", [128, 1024], "float32"),
+    "l1": ("sbuf", [128, 7 * 128], "float32"),
+    "l2": ("sbuf", [128, 7 * 32], "float32"),
+    "l3": ("sbuf", [128, 16], "float32"),
+    "l4": ("sbuf", [128, 2 * 4], "float32"),
+    "l5": ("sbuf", [128, 2 * 2], "float32"),
+}
+SEMAPHORES = ["ld", "s1", "s2", "s3", "s4", "s5", "sent", "fin"]
+
+
+def block_of(j, u):
+    if j in PORT:
+        return 2 * PORT.index(j) + u
+    return 2 * PLAIN.index(j) + (1 - u)
+
+
+def hand_out(h):
+    cable = [2 * m for m in range(4)]
+    cable[PORT[h] // 2] = PORT[h]
+    cable[PORT[3 - h] // 2] = PORT[3 - h] ^ 1
+    return cable, [c ^ 1 for c in cable]
+
+
+def rank_program(g, core, T, topo):
+    h0, k0, j0 = topo.host(core), topo.chip(core), core % 8
+    par, k2 = k0 & 1, k0 >> 1
+    u, w0 = k2 >> 2, k2 & 3
+    sem = T.sem
+    sent = [0]
+
+    def world(h, k, j):
+        return 128 * h + 8 * k + j
+
+    def send(items, remote_sem, engines):
+        transfers = []
+        for n, (dst, out, srcs) in enumerate(items):
+            rid, pid = topo.addr(dst, core)
+            mask = ((1 << engines) - 1) << (n * engines)
+            where = dict(dst_ids=[bass.DstId(rid=rid, pnc=pid)], dma_engine_mask=mask, remote_sem=remote_sem)
+            if len(srcs) == 1:
+                transfers.append(bass.RemoteDMATransfer(src=srcs[0], dst=out, alu_op=0, **where))
+            else:
+                transfers.append(bass.RemoteDMATransfer(srcs=srcs, dsts=[out], alu_op=1, **where))
+            sent[0] += engines
+        g.remote_dma_fused(transfers, local_sem=sem.sent)
+
+    g.dma_start(T.xs[:], T.x[:]).then_inc(sem.ld, 16)
+    g.wait_ge(sem.ld, 16)
+
+    items = []
+    for t in range(8):
+        if t != j0:
+            b, slot = block_of(t, u), (j0 if j0 < t else j0 - 1)
+            items.append((world(h0, k0, t), T.l1[:, 128 * slot:128 * slot + 128], [T.xs[:, 128 * b:128 * b + 128]]))
+    send(items, sem.s1, 1)
+    g.wait_ge(sem.s1, 7)
+
+    b0 = block_of(j0, u)
+    tgt, v = b0 >> 1, b0 & 1
+
+    def chip_parts(off, n):
+        return [T.xs[:, 128 * b0 + off:128 * b0 + off + n]] + [T.l1[:, 128 * s + off:128 * s + off + n] for s in range(7)]
+
+    items = []
+    for w in range(4):
+        q = 4 * v + w
+        if q != k2:
+            slot = k2 if k2 < q else k2 - 1
+            items.append((world(h0, 2 * q + par, PORT[tgt]), T.l2[:, 32 * slot:32 * slot + 32], chip_parts(32 * w, 32)))
+    send(items, sem.s2, 2)
+
+    if j0 in PORT:
+        g.wait_ge(sem.s2, 7 * 2)
+
+        def plane_parts(p, off, n):
+            a = 16 * p + off
+            return chip_parts(32 * w0 + a, n) + [T.l2[:, 32 * s + a:32 * s + a + n] for s in range(7)]
+
+        send([(world(h0, k0 ^ 1, j0), T.l3[:, 0:16], plane_parts(1 - par, 0, 16))], sem.s3, 8)
+        g.wait_ge(sem.s3, 8)
+
+        there = h0 if tgt in (h0, 3 - h0) else h0 ^ 1
+        cable, home = hand_out(there)
+        items = []
+        for m in range(4):
+            d = home[m ^ 1] if tgt == there else cable[m]
+            slot = 0 if there == h0 else 1
+            items.append((world(there, k0, d), T.l4[:, 4 * slot:4 * slot + 4],
+                          plane_parts(par, 4 * m, 4) + [T.l3[:, 4 * m:4 * m + 4]]))
+        send(items, sem.s4, 2)
+
+    g.wait_ge(sem.s4, 2 * 2)
+    cable, home = hand_out(h0)
+    m = j0 >> 1
+    if j0 == cable[m]:
+        owners, slot = [world(3 - h0, k0, 2 * m + i) for i in range(2)], 1
+    else:
+        owners, slot = [world(h0, k0, 2 * (m ^ 1) + i) for i in range(2)], 0
+    send([(o, T.l5[:, 2 * slot:2 * slot + 2], [T.l4[:, 2 * i:2 * i + 2], T.l4[:, 4 + 2 * i:4 + 2 * i + 2]])
+          for i, o in enumerate(owners)], sem.s5, 4)
+
+    g.wait_ge(sem.s5, 2 * 4)
+    g.dma_start(T.l5[:, 0:2], T.l5[:, 2:4], accum_op=AluOpType.add).then_inc(sem.fin, 16)
+    g.wait_ge(sem.fin, 16)
+    g.dma_start(T.y[:], T.l5[:, 0:2]).then_inc(sem.fin, 16)
+    g.wait_ge(sem.fin, 32)
+    g.wait_ge(sem.sent, sent[0])

@@ -59,8 +59,8 @@ def rank_program(g, core, T, topo):
         if t != j0:
             b, slot = block_of(t, u), (j0 if j0 < t else j0 - 1)
             items.append((world(h0, k0, t), T.l1[:, 128 * slot:128 * slot + 128], [T.xs[:, 128 * b:128 * b + 128]]))
-    send(items, sem.s1, 1)
-    g.wait_ge(sem.s1, 7)
+    send(items, sem.s1, 2)
+    g.wait_ge(sem.s1, 7 * 2)
 
     b0 = block_of(j0, u)
     tgt, v = b0 >> 1, b0 & 1

import concourse.bass as bass
from concourse.mybir import AluOpType

PORT = (2, 3, 6, 7)
PLAIN = (0, 1, 4, 5)

SCRATCH = {
    "xs": ("sbuf", [128, 1024], "float32"),
    "l1": ("sbuf", [128, 7 * 128], "float32"),
    "l2": ("sbuf", [128, 7 * 32], "float32"),
    "l3": ("sbuf", [128, 16], "float32"),
    "l4": ("sbuf", [128, 2 * 4], "float32"),
    "l5": ("sbuf", [128, 2 * 2], "float32"),
}
SEMAPHORES = ["ld", "s1", "s2", "s3", "s4", "s5", "sent", "fin"]


def block_of(j, u):
    if j in PORT:
        return 2 * PORT.index(j) + u
    return 2 * PLAIN.index(j) + (1 - u)


def hand_out(h):
    cable = [2 * m for m in range(4)]
    cable[PORT[h] // 2] = PORT[h]
    cable[PORT[3 - h] // 2] = PORT[3 - h] ^ 1
    return cable, [c ^ 1 for c in cable]


def rank_program(g, core, T, topo):
    h0, k0, j0 = topo.host(core), topo.chip(core), core % 8
    par, k2 = k0 & 1, k0 >> 1
    u, w0 = k2 >> 2, k2 & 3
    sem = T.sem
    sent = [0]

    def world(h, k, j):
        return 128 * h + 8 * k + j

    def send(items, remote_sem, engines):
        transfers = []
        for n, (dst, out, srcs) in enumerate(items):
            rid, pid = topo.addr(dst, core)
            mask = ((1 << engines) - 1) << (n * engines)
            where = dict(dst_ids=[bass.DstId(rid=rid, pnc=pid)], dma_engine_mask=mask, remote_sem=remote_sem)
            if len(srcs) == 1:
                transfers.append(bass.RemoteDMATransfer(src=srcs[0], dst=out, alu_op=0, **where))
            else:
                transfers.append(bass.RemoteDMATransfer(srcs=srcs, dsts=[out], alu_op=1, **where))
            sent[0] += engines
        g.remote_dma_fused(transfers, local_sem=sem.sent)

    g.dma_start(T.xs[:], T.x[:]).then_inc(sem.ld, 16)
    g.wait_ge(sem.ld, 16)

    items = []
    for t in range(8):
        if t != j0:
            b, slot = block_of(t, u), (j0 if j0 < t else j0 - 1)
            items.append((world(h0, k0, t), T.l1[:, 128 * slot:128 * slot + 128], [T.xs[:, 128 * b:128 * b + 128]]))
    send(items, sem.s1, 2)
    g.wait_ge(sem.s1, 7 * 2)

    b0 = block_of(j0, u)
    tgt, v = b0 >> 1, b0 & 1

    def chip_parts(off, n):
        return [T.xs[:, 128 * b0 + off:128 * b0 + off + n]] + [T.l1[:, 128 * s + off:128 * s + off + n] for s in range(7)]

    items = []
    for w in range(4):
        q = 4 * v + w
        if q != k2:
            slot = k2 if k2 < q else k2 - 1
            items.append((world(h0, 2 * q + par, PORT[tgt]), T.l2[:, 32 * slot:32 * slot + 32], chip_parts(32 * w, 32)))
    send(items, sem.s2, 2)

    if j0 in PORT:
        g.wait_ge(sem.s2, 7 * 2)

        def plane_parts(p, off, n):
            a = 16 * p + off
            return chip_parts(32 * w0 + a, n) + [T.l2[:, 32 * s + a:32 * s + a + n] for s in range(7)]

        send([(world(h0, k0 ^ 1, j0), T.l3[:, 0:16], plane_parts(1 - par, 0, 16))], sem.s3, 8)
        g.wait_ge(sem.s3, 8)

        there = h0 if tgt in (h0, 3 - h0) else h0 ^ 1
        cable, home = hand_out(there)
        items = []
        for m in range(4):
            d = home[m ^ 1] if tgt == there else cable[m]
            slot = 0 if there == h0 else 1
            items.append((world(there, k0, d), T.l4[:, 4 * slot:4 * slot + 4],
                          plane_parts(par, 4 * m, 4) + [T.l3[:, 4 * m:4 * m + 4]]))
        send(items, sem.s4, 2)

    g.wait_ge(sem.s4, 2 * 2)
    cable, home = hand_out(h0)
    m = j0 >> 1
    if j0 == cable[m]:
        owners, slot = [world(3 - h0, k0, 2 * m + i) for i in range(2)], 1
    else:
        owners, slot = [world(h0, k0, 2 * (m ^ 1) + i) for i in range(2)], 0
    send([(o, T.l5[:, 2 * slot:2 * slot + 2], [T.l4[:, 2 * i:2 * i + 2], T.l4[:, 4 + 2 * i:4 + 2 * i + 2]])
          for i, o in enumerate(owners)], sem.s5, 4)

    g.wait_ge(sem.s5, 2 * 4)
    g.dma_start(T.l5[:, 0:2], T.l5[:, 2:4], accum_op=AluOpType.add).then_inc(sem.fin, 16)
    g.wait_ge(sem.fin, 16)
    g.dma_start(T.y[:], T.l5[:, 0:2]).then_inc(sem.fin, 16)
    g.wait_ge(sem.fin, 32)
    g.wait_ge(sem.sent, sent[0])
